import numpy as np
import ml_dtypes


def mxq(x, axis, fmt="e4m3"):
    dtype, down = {"e4m3": (ml_dtypes.float8_e4m3fn, 7), "e5m2": (ml_dtypes.float8_e5m2, 14)}[fmt]
    v = np.moveaxis(np.asarray(x, np.float32).astype(ml_dtypes.bfloat16).astype(np.float64), axis, -1)
    blocks = v.reshape(v.shape[:-1] + (-1, 32))
    amax = np.abs(blocks).max(-1, keepdims=True)
    byte = np.maximum(np.where(amax > 0, np.frexp(amax)[1] - 1 + 127, 0) - down, 1)
    scale = np.exp2(byte - 127.0)
    codes = (blocks / scale).astype(np.float32).astype(dtype).astype(np.float64)
    return np.moveaxis((codes * scale).reshape(v.shape), -1, axis)


WIDE = False


def mx_kscale(k):
    if not WIDE:
        return np.ones(k)
    levels = np.array([10, -10, 5, -5, 0])
    if k % 512:
        return np.exp2(np.random.permutation(np.resize(levels, k // 32))).repeat(32)
    a = np.empty((k // 512, 16))
    for p in range(k // 512):
        a[p, :8] = np.random.permutation(np.resize(levels, 8))
        for g in range(8):
            far = levels[np.abs(levels - a[p, g]) >= 10]
            a[p, g + 8] = far[np.random.randint(len(far))]
    return np.exp2(a.ravel()).repeat(32)


BF16 = ml_dtypes.bfloat16


def bf(x):
    return np.asarray(x, np.float32).astype(BF16)


def f64(x):
    return np.asarray(x).astype(np.float64)


E2M1 = np.array([0.0, 0.5, 1.0, 1.5, 2.0, 3.0, 4.0, 6.0, -0.0, -0.5, -1.0, -1.5, -2.0, -3.0, -4.0, -6.0])


def pack_weight(w, fmt):
    k, n = w.shape
    w = f64(bf(w)).reshape(k // 32, 32, n)
    amax = np.abs(w).max(1)
    if fmt == "e4m3":
        byte = np.frexp(amax)[1] - 1 + 127 - 7
    else:
        mant, ex = np.frexp(amax / 6.0)
        byte = np.where(mant > 0.5, ex, ex - 1) + 127
    byte = np.clip(np.where(amax > 0, byte, 1), 1, 254)
    scaled = (w * np.exp2(127.0 - byte)[:, None, :]).reshape(k, n).astype(np.float32)
    by_word = np.ascontiguousarray(scaled.reshape(k // 512, 128, 4, n).transpose(0, 1, 3, 2))
    if fmt == "e4m3":
        words = by_word.astype(ml_dtypes.float8_e4m3fn).view(np.uint8)
    else:
        c = by_word.astype(ml_dtypes.float4_e2m1fn).view(np.uint8) & 0xF
        words = c[..., 0::2] | (c[..., 1::2] << 4)
    return np.ascontiguousarray(words), np.ascontiguousarray(byte.astype(np.uint8).reshape(k // 512, 16, n))


def unpack_weight(words, scales, fmt):
    g, p, n, _ = words.shape
    if fmt == "e4m3":
        vals = np.ascontiguousarray(words).view(ml_dtypes.float8_e4m3fn).astype(np.float64)
    else:
        nib = np.empty((g, p, n, 4), np.uint8)
        nib[..., 0::2] = words & 0xF
        nib[..., 1::2] = words >> 4
        vals = E2M1[nib]
    vals = vals * np.repeat(np.exp2(scales.astype(np.float64) - 127.0), 8, axis=1)[..., None]
    return vals.transpose(0, 1, 3, 2).reshape(g * 512, n)
def pack4(w):
    words, scales = pack_weight(w, "e2m1")
    return words.reshape(words.shape[0], 128, -1), scales


def unpack4(words, scales):
    return unpack_weight(words.reshape(words.shape[0], 128, -1, 2), scales, "e2m1")


def planes(Y):
    n, m = Y.shape
    b = f64(bf(Y)).reshape(n // 32, 32, m)
    amax = np.abs(b).max(1)
    byte = np.clip(np.where(amax > 0, np.frexp(amax)[1] - 1 + 127 - 7, 1), 1, 254)
    codes = (b * np.exp2(127.0 - byte)[:, None, :]).reshape(n, m).astype(np.float32).astype(ml_dtypes.float8_e4m3fn).view(np.uint8)
    words = codes.reshape(n // 512, 128, 4, m).transpose(0, 1, 3, 2)
    return np.ascontiguousarray(words), np.ascontiguousarray(byte.astype(np.uint8).reshape(n // 512, 16, m))


N, M, T, P = 1024, 1024, 1024, 1024


def clip_rows(g, r, a):
    n = np.sqrt(np.sum(g * g, axis=1) + 1e-6)
    scale = np.minimum(1.0, r / n)
    return a[:, None] * g * scale[:, None]


def bounded_release(e, h):
    return h[:, None] * 2.0 * np.tanh(e / 2.0)


def setup_inputs():
    s, t = mx_kscale(N), mx_kscale(M)
    g = bf(np.random.standard_normal((N, P)))
    r = bf(np.sqrt(P) * np.random.uniform(0.5, 1.5, N))
    a = bf((1.0 + 0.1 * np.random.standard_normal(N)) * s)
    c_words, c_scales = pack4((np.random.standard_normal((M, N)) / np.sqrt(N) / s[None, :]).T)
    z = bf(np.random.standard_normal((M, P)))
    h = bf((1.0 + 0.1 * np.random.standard_normal(M)) * t)
    b_words, b_scales = pack4((np.random.standard_normal((T, M)) / np.sqrt(M) / t[None, :]).T)
    return {
        "g": g,
        "r": r,
        "a": a,
        "c_words": c_words,
        "c_scales": c_scales,
        "z": z,
        "h": h,
        "b_words": b_words,
        "b_scales": b_scales,
    }


def core(g, r, a, c_words, c_scales, z, h, b_words, b_scales):
    k = clip_rows(f64(g), f64(r), f64(a))
    e = (unpack4(c_words, c_scales).T @ mxq(k, 0, "e4m3")) + 0.5 * f64(z)
    q = bounded_release(e, f64(h))
    return unpack4(b_words, b_scales).T @ mxq(q, 0, "e4m3")


def reference(g, r, a, c_words, c_scales, z, h, b_words, b_scales):
    R_out = core(g, r, a, c_words, c_scales, z, h, b_words, b_scales)
    words, scales = planes(R_out.T)
    return R_out, words, scales

@@ -1,0 +1,370 @@
+from contextlib import ExitStack
+
+import concourse.mybir as mybir
+from concourse.masks import make_identity
+
+F32 = mybir.dt.float32
+BF16 = mybir.dt.bfloat16
+U32 = mybir.dt.uint32
+I32 = mybir.dt.int32
+U8 = mybir.dt.uint8
+E4M3 = mybir.dt.float8_e4m3fn_x4
+E2M1 = mybir.dt.float4_e2m1fn_x4
+ACT = mybir.ActivationFunctionType
+ALU = mybir.AluOpType
+
+FLOPS = 2 * 2 * 1024 * 1024 * 1024
+
+P = 128
+W = 128
+NCH = 8
+
+
+def tile_clippedmatrixmechanismboundedrelease_x2_kernel(tc, g, r, a, c_words, c_scales, z, h, b_words, b_scales, out, out_words, out_scales):
+    nc = tc.nc
+    with ExitStack() as ctx:
+        keep = ctx.enter_context(tc.tile_pool(name="keep", bufs=1))
+        work = ctx.enter_context(tc.tile_pool(name="work", bufs=2))
+        pe = ctx.enter_context(tc.psum_pool(name="pe", bufs=4))
+        pr = ctx.enter_context(tc.psum_pool(name="pr", bufs=2))
+        pw = ctx.enter_context(tc.psum_pool(name="pw", bufs=2))
+        ctx.enter_context(nc.allow_non_contiguous_dma(reason="small vectors and strided tiles"))
+
+        g_sb = keep.tile([P, 2, 4, 1024], BF16)
+        c_raw = keep.tile([P, 2, 2048], U8, align_bytes=64)
+        c_perm = keep.tile([P, 2, 2048], U8, align_bytes=64)
+        cs_raw = keep.tile([P, 2, 1024], U8, align_bytes=64)
+        cs_perm = keep.tile([P, 2, 1024], U8, align_bytes=64)
+        b_sb = keep.tile([P, 2, 2048], U8, align_bytes=64)
+        bs_sb = keep.tile([P, 2, 1024], U8, align_bytes=64)
+        z_sb = keep.tile([P, 2, 4, 1024], BF16)
+        r_sb = keep.tile([P, 2, 4], BF16)
+        a_sb = keep.tile([P, 2, 4], BF16)
+        h_sb = keep.tile([P, 2, 4], BF16)
+        h2 = keep.tile([P, 2, 4], F32)
+        ss = keep.tile([P, 2, 4], F32)
+        rn = keep.tile([P, 2, 4], F32)
+        ratio = keep.tile([P, 2, 4], F32)
+        alpha = keep.tile([P, 2, 4], F32)
+        k_codes = keep.tile([P, 4, 2, 256], U32, align_bytes=64)
+        k_scales = keep.tile([P, 4, 2, 256], U8, align_bytes=64)
+        q_codes = keep.tile([P, NCH, 2, W], U32, align_bytes=64)
+        q_scales = keep.tile([P, NCH, 2, W], U8, align_bytes=64)
+        o_sb = keep.tile([P, 8, 1024], F32)
+        ident = keep.tile([P, P], F32)
+
+        nc.vector.memset(cs_raw[:].rearrange("p g n -> p (g n)").bitcast(I32), 0)
+        for q4 in range(4):
+            nc.scalar.dma_start(
+                out=cs_raw[32 * q4 : 32 * q4 + 4, :, :].rearrange("p g n -> p (g n)").bitcast(I32).rearrange("p (g n) -> p g n", g=2),
+                in_=c_scales.bitcast(I32)[:, 4 * q4 : 4 * q4 + 4, :].rearrange("g q n -> q g n"),
+            )
+        nc.gpsimd.dma_start(out=r_sb[:], in_=r.rearrange("(i p t) -> p i t", i=2, t=4))
+        nc.gpsimd.dma_start(out=a_sb[:], in_=a.rearrange("(i p t) -> p i t", i=2, t=4))
+        nc.gpsimd.dma_start(out=h_sb[:], in_=h.rearrange("(i p t) -> p i t", i=2, t=4))
+        nc.gpsimd.memset(bs_sb[:].rearrange("p g n -> p (g n)").bitcast(I32), 0)
+        make_identity(nc, ident[:])
+
+        for i in range(2):
+            nc.sync.dma_start(out=c_raw[:, i, :].bitcast(I32), in_=c_words[i].bitcast(I32))
+        g4 = g.rearrange("(i p t) j -> i p t j", i=2, t=4)
+        for i, t0, t1 in [(0, 0, 1), (0, 1, 2), (0, 2, 4), (1, 0, 2), (1, 2, 4)]:
+            nc.sync.dma_start(out=g_sb[:, i, t0:t1, :], in_=g4[i, :, t0:t1, :])
+        z4 = z.rearrange("(i p t) j -> p i t j", i=2, t=4)
+        for i in range(2):
+            nc.sync.dma_start(out=z_sb[:, i, :, 0:512], in_=z4[:, i, :, 0:512])
+        for i in range(2):
+            nc.sync.dma_start(out=b_sb[:, i, :].bitcast(I32), in_=b_words[i].bitcast(I32))
+        for q4 in range(4):
+            nc.sync.dma_start(
+                out=bs_sb[32 * q4 : 32 * q4 + 4, :, :].rearrange("p g n -> p (g n)").bitcast(I32).rearrange("p (g n) -> p g n", g=2),
+                in_=b_scales.bitcast(I32)[:, 4 * q4 : 4 * q4 + 4, :].rearrange("g q n -> q g n"),
+            )
+        for i in range(2):
+            nc.sync.dma_start(out=z_sb[:, i, :, 512:1024], in_=z4[:, i, :, 512:1024])
+
+        for b in range(2):
+            for i in range(2):
+                cols = slice(1024 * b, 1024 * (b + 1))
+                nc.vector.tensor_copy(
+                    out=c_perm[:, i, cols].rearrange("p (t q e) -> p t q e", t=4, e=2),
+                    in_=c_raw[:, i, cols].rearrange("p (q t e) -> p t q e", t=4, e=2),
+                )
+
+        def sumsq_s(i, t):
+            sq_s = work.tile([P, 1024], BF16)
+            nc.scalar.activation(out=sq_s[:], in_=g_sb[:, i, t, :], func=ACT.Square, accum_out=ss[:, i, t : t + 1])
+
+        def sumsq_v(i, t):
+            sq_v = work.tile([P, 1024], F32)
+            nc.vector.scalar_tensor_tensor(
+                out=sq_v[:], in0=g_sb[:, i, t, :], scalar=1.0, in1=g_sb[:, i, t, :], op0=ALU.mult, op1=ALU.mult, accum_out=ss[:, i, t : t + 1]
+            )
+
+        def norms(i):
+            nc.scalar.activation(out=rn[:, i, :], in_=ss[:, i, :], func=ACT.Abs_reciprocal_sqrt, bias=1e-6)
+            nc.vector.tensor_tensor(out=ratio[:, i, :], in0=rn[:, i, :], in1=r_sb[:, i, :], op=ALU.mult)
+            nc.vector.scalar_tensor_tensor(out=alpha[:, i, :], in0=ratio[:, i, :], scalar=1.0, in1=a_sb[:, i, :], op0=ALU.min, op1=ALU.mult)
+
+        ki = {}
+
+        def k_tile(qr):
+            k_in = work.tile([P, 2, 256, 4], BF16, align_bytes=64)
+            ki[qr] = k_in
+
+        def k_fused(qr, i):
+            nc.vector.tensor_tensor(
+                out=ki[qr][:, i, :, :],
+                in0=g_sb[:, i, :, 256 * qr : 256 * (qr + 1)].rearrange("p t j -> p j t"),
+                in1=alpha[:, i, :].unsqueeze(1).to_broadcast([P, 256, 4]),
+                op=ALU.mult,
+            )
+
+        kc = {}
+
+        def k_scale(i, j0, width):
+            k_c = work.tile([P, 4, 512], BF16)
+            for t in range(4):
+                nc.vector.tensor_scalar(
+                    out=k_c[:, t, 0:width], in0=g_sb[:, i, t, j0 : j0 + width], scalar1=alpha[:, i, t : t + 1], scalar2=None, op0=ALU.mult
+                )
+            for j in range(0, width, 256):
+                kc[(i, (j0 + j) // 256)] = k_c[:, :, j : j + 256]
+
+        def k_inter(qr, i):
+            nc.scalar.copy(out=ki[qr][:, i, :, :], in_=kc[(i, qr)].rearrange("p t j -> p j t"))
+
+        def k_quant(qr, i0, i1):
+            nc.vector.quantize_mx(
+                out=k_codes[:, qr, i0:i1, :].rearrange("p i j -> p (i j)").bitcast(E4M3),
+                scales=k_scales[:, qr, i0:i1, :].rearrange("p i j -> p (i j)"),
+                in_=ki[qr][:, i0:i1, :, :].rearrange("p i j t -> p (i j t)"),
+            )
+
+        eb = {}
+
+        def enc(c):
+            cols = slice(W * (c % 2), W * (c % 2 + 1))
+            for b in range(2):
+                e_ps = pe.tile([P, 4, W], F32)
+                eb[(c, b)] = e_ps
+                for t in range(4):
+                    m0 = 512 * b + 128 * t
+                    for i in range(2):
+                        nc.tensor.matmul_mx(
+                            out=e_ps[:, t, :],
+                            lhsT=c_perm[:, i, 2 * m0 : 2 * m0 + 256].bitcast(E2M1),
+                            lhsT_scale=cs_perm[:, i, m0 : m0 + 128],
+                            rhs=k_codes[:, c // 2, i, cols].bitcast(E4M3),
+                            rhs_scale=k_scales[:, c // 2, i, cols],
+                            start=(i == 0),
+                            stop=(i == 1),
+                        )
+
+        et = {}
+
+        def noise(c):
+            cols = slice(W * c, W * (c + 1))
+            e_sb = work.tile([P, 2, W, 4], F32)
+            et[c] = e_sb
+            for b in range(2):
+                nc.vector.scalar_tensor_tensor(
+                    out=e_sb[:, b, :, :],
+                    in0=z_sb[:, b, :, cols].rearrange("p t j -> p j t"),
+                    scalar=0.5,
+                    in1=eb[(c, b)][:].rearrange("p t j -> p j t"),
+                    op0=ALU.mult,
+                    op1=ALU.add,
+                )
+
+        th = {}
+
+        def bound(c):
+            t_sb = work.tile([P, 2, W, 4], F32)
+            th[c] = t_sb
+            nc.scalar.activation(out=t_sb[:], in_=et[c][:], func=ACT.Tanh, scale=0.5)
+
+        qt = {}
+
+        def gain(c):
+            q_sb = work.tile([P, 2, W, 4], BF16, align_bytes=64)
+            qt[c] = q_sb
+            nc.vector.tensor_tensor(out=q_sb[:], in0=th[c][:], in1=h2[:].unsqueeze(2).to_broadcast([P, 2, W, 4]), op=ALU.mult)
+
+        def q_quant(c):
+            nc.vector.quantize_mx(
+                out=q_codes[:, c, :, :].rearrange("p b j -> p (b j)").bitcast(E4M3),
+                scales=q_scales[:, c, :, :].rearrange("p b j -> p (b j)"),
+                in_=qt[c][:].rearrange("p b j t -> p (b j t)"),
+            )
+
+        rb = {}
+
+        def dec(c, u):
+            r_ps = pr.tile([P, 4, W], F32)
+            rb[(c, u)] = r_ps
+            for v in range(4):
+                n0 = 128 * (4 * u + v)
+                for b in range(2):
+                    nc.tensor.matmul_mx(
+                        out=r_ps[:, v, :],
+                        lhsT=b_sb[:, b, 2 * n0 : 2 * n0 + 256].bitcast(E2M1),
+                        lhsT_scale=bs_sb[:, b, n0 : n0 + 128],
+                        rhs=q_codes[:, c, b, :].bitcast(E4M3),
+                        rhs_scale=q_scales[:, c, b, :],
+                        start=(b == 0),
+                        stop=(b == 1),
+                    )
+
+        def leave(c, u, on_vector=False):
+            dst = o_sb[:, 4 * u : 4 * u + 4, W * c : W * (c + 1)]
+            if on_vector:
+                nc.vector.tensor_copy(out=dst, in_=rb[(c, u)][:])
+            else:
+                nc.scalar.copy(out=dst, in_=rb[(c, u)][:])
+
+        out3 = out.rearrange("(v p) j -> p v j", p=P)
+
+        def store(j0, j1, v0=0, v1=8):
+            nc.sync.dma_start(out=out3[:, v0:v1, j0:j1], in_=o_sb[:, v0:v1, j0:j1])
+
+        pt = {}
+        pc = {}
+
+        def p_tile(half):
+            p_sb = work.tile([P, 8, 128, 4], BF16, align_bytes=64)
+            pt[half] = p_sb
+            p_codes = work.tile([P, 1024], U32, align_bytes=64)
+            p_scales = work.tile([P, 1024], U8, align_bytes=64)
+            pc[half] = (p_codes, p_scales)
+
+        def turn_f32(half, v, on_vector=False):
+            w_ps = pw.tile([P, 4, P], F32)
+            for t in range(4):
+                nc.tensor.transpose(w_ps[:, t, :], o_sb[:, v, 512 * half + t : 512 * (half + 1) : 4], ident[:])
+            dst = pt[half][:, v, :, :]
+            src = w_ps[:].rearrange("p t m -> p m t")
+            if on_vector:
+                nc.vector.tensor_copy(out=dst, in_=src)
+            else:
+                nc.scalar.copy(out=dst, in_=src)
+
+        o_bf = keep.tile([P, 8, 512], BF16)
+
+        def cast(c, u0, u1):
+            j0 = W * (c % 4)
+            nc.vector.tensor_copy(out=o_bf[:, 4 * u0 : 4 * u1, j0 : j0 + W], in_=o_sb[:, 4 * u0 : 4 * u1, W * c : W * (c + 1)])
+
+        def turn_words(half, v2, on_vector=False):
+            words = o_bf[:].bitcast(F32)
+            w_ps = pw.tile([P, 4, P], F32)
+            for v in range(2):
+                for e in range(2):
+                    nc.tensor.transpose(w_ps[:, 2 * v + e, :], words[:, 2 * v2 + v, e::2], ident[:])
+            dst = pt[half][:, 2 * v2 : 2 * v2 + 2, :, :].rearrange("p v m t -> p (v m t)").bitcast(F32).rearrange("p (v m e) -> p v m e", v=2, e=2)
+            src = w_ps[:].rearrange("p (v e) m -> p v m e", v=2)
+            if on_vector:
+                nc.vector.tensor_copy(out=dst, in_=src)
+            else:
+                nc.scalar.copy(out=dst, in_=src)
+
+        def p_quant(half, v0, v1):
+            codes, scales = pc[half]
+            cols = slice(128 * v0, 128 * v1)
+            nc.vector.quantize_mx(
+                out=codes[:, cols].bitcast(E4M3), scales=scales[:, cols], in_=pt[half][:, v0:v1, :, :].rearrange("p v m t -> p (v m t)")
+            )
+
+        def p_store(half, v0, v1):
+            cols = slice(128 * v0, 128 * v1)
+            nc.sync.dma_start(out=out_words[half].rearrange("p m t -> p (m t)").bitcast(I32)[:, cols], in_=pc[half][0][:, cols].bitcast(I32))
+
+        def p_scales_out(half):
+            for q4 in range(4):
+                nc.sync.dma_start(
+                    out=out_scales.bitcast(I32)[half, 4 * q4 : 4 * q4 + 4, :],
+                    in_=pc[half][1][32 * q4 : 32 * q4 + 4, :].bitcast(I32),
+                )
+
+        SV = {(0,1),(0,3),(1,2)}
+        for i in range(2):
+            for t in range(4):
+                if (i, t) in SV:
+                    sumsq_v(i, t)
+                else:
+                    sumsq_s(i, t)
+            norms(i)
+        for b in range(2):
+            cols = slice(512 * b, 512 * (b + 1))
+            nc.vector.tensor_copy(
+                out=cs_perm[:, :, cols].rearrange("p i (t q) -> p i t q", t=4),
+                in_=cs_raw[:, :, cols].rearrange("p i (q t) -> p i t q", t=4),
+            )
+        nc.vector.tensor_scalar(out=h2[:], in0=h_sb[:], scalar1=2.0, scalar2=None, op0=ALU.mult)
+        KF = {(0,0)}
+        LV = {(6,1),(7,1)}
+        TV = {(1,1),(1,3)}
+        WORDS = (1,)
+
+        def k_prep(qr):
+            k_tile(qr)
+            for i in range(2):
+                if (qr, i) in KF:
+                    k_fused(qr, i)
+                else:
+                    if qr % 2 == 0 or (qr - 1, i) in KF:
+                        k_scale(i, 256 * qr, 512 if qr % 2 == 0 and (qr + 1, i) not in KF else 256)
+                    k_inter(qr, i)
+            if qr == 0:
+                k_quant(0, 0, 1)
+                k_quant(0, 1, 2)
+            else:
+                k_quant(qr, 0, 2)
+
+        k_prep(0)
+        enc(0)
+        k_prep(1)
+        p_tile(0)
+        p_tile(1)
+        for s in range(0, 11):
+            if s + 1 < NCH:
+                enc(s + 1)
+            if s < NCH:
+                noise(s)
+            if 0 <= s - 2 < NCH:
+                dec(s - 2, 0)
+                leave(s - 2, 0, (s - 2, 0) in LV)
+                dec(s - 2, 1)
+            if s < NCH:
+                bound(s)
+            if 0 <= s - 2 < NCH:
+                leave(s - 2, 1, (s - 2, 1) in LV)
+            if s in (0, 2):
+                k_prep(2 + s // 2)
+            if 0 <= s - 1 < NCH:
+                gain(s - 1)
+                q_quant(s - 1)
+            c = s - 2
+            if 0 <= c < NCH and c // 4 in WORDS:
+                cast(c, 0, 1)
+                cast(c, 1, 2)
+            if c in (1, 3, 5):
+                store(W * (c - 1), W * (c + 1))
+            if c in (6, 7):
+                store(W * c, W * (c + 1))
+            if c in (3, 7):
+                half = c // 4
+                if half in WORDS:
+                    for v2 in range(4):
+                        turn_words(half, v2, (half, v2) in TV)
+                        if half == 1 or v2 % 2 == 1:
+                            p_quant(half, 2 * v2 if half == 1 else 2 * v2 - 2, 2 * v2 + 2)
+                        if v2 % 2 == 1:
+                            p_store(half, 2 * v2 - 2, 2 * v2 + 2)
+                else:
+                    for v in range(8):
+                        turn_f32(half, v, (half, v) in TV)
+                        if v % 4 == 3:
+                            p_quant(half, v - 3, v + 1)
+                            p_store(half, v - 3, v + 1)
+                p_scales_out(half)

@@ -25,10 +25,11 @@ def tile_clippedmatrixmechanismboundedrelease_x2_kernel(tc, g, r, a, c_words, c_
     with ExitStack() as ctx:
         keep = ctx.enter_context(tc.tile_pool(name="keep", bufs=1))
         work = ctx.enter_context(tc.tile_pool(name="work", bufs=2))
-        pe = ctx.enter_context(tc.psum_pool(name="pe", bufs=4))
+        pe = ctx.enter_context(tc.psum_pool(name="pe", bufs=3))
         pr = ctx.enter_context(tc.psum_pool(name="pr", bufs=2))
-        pw = ctx.enter_context(tc.psum_pool(name="pw", bufs=2))
+        pw = ctx.enter_context(tc.psum_pool(name="pw", bufs=3))
         ctx.enter_context(nc.allow_non_contiguous_dma(reason="small vectors and strided tiles"))
+        ctx.enter_context(tc.manual_schedule())
 
         g_sb = keep.tile([P, 2, 4, 1024], BF16)
         c_raw = keep.tile([P, 2, 2048], U8, align_bytes=64)
@@ -54,42 +55,36 @@ def tile_clippedmatrixmechanismboundedrelease_x2_kernel(tc, g, r, a, c_words, c_
         ident = keep.tile([P, P], F32)
 
         nc.vector.memset(cs_raw[:].rearrange("p g n -> p (g n)").bitcast(I32), 0)
-        for q4 in range(4):
-            nc.scalar.dma_start(
-                out=cs_raw[32 * q4 : 32 * q4 + 4, :, :].rearrange("p g n -> p (g n)").bitcast(I32).rearrange("p (g n) -> p g n", g=2),
-                in_=c_scales.bitcast(I32)[:, 4 * q4 : 4 * q4 + 4, :].rearrange("g q n -> q g n"),
-            )
         nc.gpsimd.dma_start(out=r_sb[:], in_=r.rearrange("(i p t) -> p i t", i=2, t=4))
         nc.gpsimd.dma_start(out=a_sb[:], in_=a.rearrange("(i p t) -> p i t", i=2, t=4))
         nc.gpsimd.dma_start(out=h_sb[:], in_=h.rearrange("(i p t) -> p i t", i=2, t=4))
         nc.gpsimd.memset(bs_sb[:].rearrange("p g n -> p (g n)").bitcast(I32), 0)
         make_identity(nc, ident[:])
 
-        for i in range(2):
-            nc.sync.dma_start(out=c_raw[:, i, :].bitcast(I32), in_=c_words[i].bitcast(I32))
+        def load_words(dst, src, i):
+            nc.sync.dma_start(out=dst[:, i, :].bitcast(I32), in_=src[i].bitcast(I32))
+
+        def load_scales(dst, src):
+            for q4 in range(4):
+                nc.sync.dma_start(
+                    out=dst[32 * q4 : 32 * q4 + 4, :, :].rearrange("p g n -> p (g n)").bitcast(I32).rearrange("p (g n) -> p g n", g=2),
+                    in_=src.bitcast(I32)[:, 4 * q4 : 4 * q4 + 4, :].rearrange("g q n -> q g n"),
+                )
+
         g4 = g.rearrange("(i p t) j -> i p t j", i=2, t=4)
+        z4 = z.rearrange("(i p t) j -> p i t j", i=2, t=4)
+        load_words(c_raw, c_words, 0)
         for i, t0, t1 in [(0, 0, 1), (0, 1, 2), (0, 2, 4), (1, 0, 2), (1, 2, 4)]:
             nc.sync.dma_start(out=g_sb[:, i, t0:t1, :], in_=g4[i, :, t0:t1, :])
-        z4 = z.rearrange("(i p t) j -> p i t j", i=2, t=4)
+        load_words(c_raw, c_words, 1)
+        load_scales(cs_raw, c_scales)
         for i in range(2):
             nc.sync.dma_start(out=z_sb[:, i, :, 0:512], in_=z4[:, i, :, 0:512])
         for i in range(2):
-            nc.sync.dma_start(out=b_sb[:, i, :].bitcast(I32), in_=b_words[i].bitcast(I32))
-        for q4 in range(4):
-            nc.sync.dma_start(
-                out=bs_sb[32 * q4 : 32 * q4 + 4, :, :].rearrange("p g n -> p (g n)").bitcast(I32).rearrange("p (g n) -> p g n", g=2),
-                in_=b_scales.bitcast(I32)[:, 4 * q4 : 4 * q4 + 4, :].rearrange("g q n -> q g n"),
-            )
+            load_words(b_sb, b_words, i)
+        load_scales(bs_sb, b_scales)
         for i in range(2):
             nc.sync.dma_start(out=z_sb[:, i, :, 512:1024], in_=z4[:, i, :, 512:1024])
-
-        for b in range(2):
-            for i in range(2):
-                cols = slice(1024 * b, 1024 * (b + 1))
-                nc.vector.tensor_copy(
-                    out=c_perm[:, i, cols].rearrange("p (t q e) -> p t q e", t=4, e=2),
-                    in_=c_raw[:, i, cols].rearrange("p (q t e) -> p t q e", t=4, e=2),
-                )
 
         def sumsq_s(i, t):
             sq_s = work.tile([P, 1024], BF16)
@@ -109,7 +104,7 @@ def tile_clippedmatrixmechanismboundedrelease_x2_kernel(tc, g, r, a, c_words, c_
         ki = {}
 
         def k_tile(qr):
-            k_in = work.tile([P, 2, 256, 4], BF16, align_bytes=64)
+            k_in = keep.tile([P, 2, 256, 4], BF16, align_bytes=64, bufs=4)
             ki[qr] = k_in
 
         def k_fused(qr, i):
@@ -123,7 +118,7 @@ def tile_clippedmatrixmechanismboundedrelease_x2_kernel(tc, g, r, a, c_words, c_
         kc = {}
 
         def k_scale(i, j0, width):
-            k_c = work.tile([P, 4, 512], BF16)
+            k_c = keep.tile([P, 4, 512], BF16, bufs=4)
             for t in range(4):
                 nc.vector.tensor_scalar(
                     out=k_c[:, t, 0:width], in0=g_sb[:, i, t, j0 : j0 + width], scalar1=alpha[:, i, t : t + 1], scalar2=None, op0=ALU.mult
@@ -286,85 +281,136 @@ def tile_clippedmatrixmechanismboundedrelease_x2_kernel(tc, g, r, a, c_words, c_
                     in_=pc[half][1][32 * q4 : 32 * q4 + 4, :].bitcast(I32),
                 )
 
-        SV = {(0,1),(0,3),(1,2)}
-        for i in range(2):
-            for t in range(4):
-                if (i, t) in SV:
-                    sumsq_v(i, t)
-                else:
-                    sumsq_s(i, t)
-            norms(i)
-        for b in range(2):
+        def c_order(i, b):
+            cols = slice(1024 * b, 1024 * (b + 1))
+            nc.vector.tensor_copy(
+                out=c_perm[:, i, cols].rearrange("p (t q e) -> p t q e", t=4, e=2),
+                in_=c_raw[:, i, cols].rearrange("p (q t e) -> p t q e", t=4, e=2),
+            )
+
+        def cs_order(b):
             cols = slice(512 * b, 512 * (b + 1))
             nc.vector.tensor_copy(
                 out=cs_perm[:, :, cols].rearrange("p i (t q) -> p i t q", t=4),
                 in_=cs_raw[:, :, cols].rearrange("p i (q t) -> p i t q", t=4),
             )
+
+        def norm_root(i):
+            nc.scalar.activation(out=rn[:, i, :], in_=ss[:, i, :], func=ACT.Abs_reciprocal_sqrt, bias=1e-6)
+
+        def norm_ratio(i):
+            nc.vector.tensor_tensor(out=ratio[:, i, :], in0=rn[:, i, :], in1=r_sb[:, i, :], op=ALU.mult)
+
+        def norm_alpha(i):
+            nc.vector.scalar_tensor_tensor(out=alpha[:, i, :], in0=ratio[:, i, :], scalar=1.0, in1=a_sb[:, i, :], op0=ALU.min, op1=ALU.mult)
+
+        c_order(0, 0)
+        sumsq_s(0, 0)
+        sumsq_v(0, 1)
+        sumsq_s(0, 2)
+        sumsq_v(0, 3)
+        c_order(0, 1)
+        norm_root(0)
+        sumsq_s(1, 0)
+        norm_ratio(0)
+        sumsq_v(1, 2)
+        norm_alpha(0)
+        sumsq_s(1, 1)
+        sumsq_s(1, 3)
+        norm_root(1)
         nc.vector.tensor_scalar(out=h2[:], in0=h_sb[:], scalar1=2.0, scalar2=None, op0=ALU.mult)
-        KF = {(0,0)}
-        LV = {(6,1),(7,1)}
-        TV = {(1,1),(1,3)}
-        WORDS = (1,)
-
-        def k_prep(qr):
-            k_tile(qr)
-            for i in range(2):
-                if (qr, i) in KF:
-                    k_fused(qr, i)
-                else:
-                    if qr % 2 == 0 or (qr - 1, i) in KF:
-                        k_scale(i, 256 * qr, 512 if qr % 2 == 0 and (qr + 1, i) not in KF else 256)
-                    k_inter(qr, i)
-            if qr == 0:
-                k_quant(0, 0, 1)
-                k_quant(0, 1, 2)
-            else:
-                k_quant(qr, 0, 2)
-
-        k_prep(0)
-        enc(0)
-        k_prep(1)
+        k_tile(0)
+        k_tile(1)
+        k_tile(2)
+        k_tile(3)
+        k_fused(0, 0)
+        c_order(1, 0)
+        norm_ratio(1)
+        cs_order(0)
+        norm_alpha(1)
+        k_quant(0, 0, 1)
+        k_scale(1, 0, 512)
+        k_inter(0, 1)
+        k_scale(0, 256, 256)
+        c_order(1, 1)
+        cs_order(1)
+        k_quant(0, 1, 2)
+        k_scale(0, 512, 512)
+        k_scale(1, 512, 512)
+        k_inter(1, 1)
+        k_inter(1, 0)
+        k_inter(2, 1)
         p_tile(0)
         p_tile(1)
-        for s in range(0, 11):
-            if s + 1 < NCH:
+        enc(0)
+        enc(1)
+
+        for s in range(0, 8):
+            noise(s)
+            if s == 0:
+                k_quant(1, 0, 2)
+            if s == 3:
+                k_quant(2, 0, 2)
+            if s == 4:
+                k_quant(3, 0, 2)
+            if 1 <= s + 1 < NCH and s >= 1:
                 enc(s + 1)
-            if s < NCH:
-                noise(s)
-            if 0 <= s - 2 < NCH:
+            if s >= 3:
+                leave(s - 3, 0)
+                leave(s - 3, 1)
+            bound(s)
+            if s == 6:
+                turn_f32(0, 0)
+            if s >= 2:
+                q_quant(s - 2)
                 dec(s - 2, 0)
-                leave(s - 2, 0, (s - 2, 0) in LV)
                 dec(s - 2, 1)
-            if s < NCH:
-                bound(s)
-            if 0 <= s - 2 < NCH:
-                leave(s - 2, 1, (s - 2, 1) in LV)
-            if s in (0, 2):
-                k_prep(2 + s // 2)
-            if 0 <= s - 1 < NCH:
+            if s in (0, 1, 2):
+                k_inter(*((3, 0), (2, 0), (3, 1))[s])
+            if s >= 1:
                 gain(s - 1)
-                q_quant(s - 1)
-            c = s - 2
-            if 0 <= c < NCH and c // 4 in WORDS:
-                cast(c, 0, 1)
-                cast(c, 1, 2)
-            if c in (1, 3, 5):
-                store(W * (c - 1), W * (c + 1))
-            if c in (6, 7):
-                store(W * c, W * (c + 1))
-            if c in (3, 7):
-                half = c // 4
-                if half in WORDS:
-                    for v2 in range(4):
-                        turn_words(half, v2, (half, v2) in TV)
-                        if half == 1 or v2 % 2 == 1:
-                            p_quant(half, 2 * v2 if half == 1 else 2 * v2 - 2, 2 * v2 + 2)
-                        if v2 % 2 == 1:
-                            p_store(half, 2 * v2 - 2, 2 * v2 + 2)
-                else:
-                    for v in range(8):
-                        turn_f32(half, v, (half, v) in TV)
-                        if v % 4 == 3:
-                            p_quant(half, v - 3, v + 1)
-                            p_store(half, v - 3, v + 1)
-                p_scales_out(half)
+            if s in (4, 6):
+                store(W * (s - 4), W * (s - 2))
+        cast(4, 0, 2)
+        leave(5, 0)
+        leave(5, 1)
+        turn_f32(0, 1)
+        q_quant(6)
+        dec(6, 0)
+        gain(7)
+        q_quant(7)
+        leave(6, 0)
+        turn_f32(0, 2, True)
+        dec(6, 1)
+        leave(6, 1)
+        dec(7, 0)
+        leave(7, 0)
+        store(W * 4, W * 6)
+        cast(5, 0, 2)
+        cast(6, 0, 1)
+        turn_f32(0, 3, True)
+        dec(7, 1)
+        cast(7, 0, 1)
+        turn_f32(0, 4)
+        p_quant(0, 0, 4)
+        p_store(0, 0, 4)
+        leave(7, 1, True)
+        store(W * 6, W * 7)
+        turn_f32(0, 5)
+        turn_words(1, 0)
+        turn_words(1, 1)
+        cast(6, 1, 2)
+        cast(7, 1, 2)
+        store(W * 7, W * 8)
+        turn_f32(0, 6, True)
+        turn_f32(0, 7)
+        p_quant(1, 0, 4)
+        p_store(1, 0, 4)
+        p_quant(0, 4, 8)
+        p_store(0, 4, 8)
+        p_scales_out(0)
+        turn_words(1, 2, True)
+        turn_words(1, 3)
+        p_quant(1, 4, 8)
+        p_store(1, 4, 8)
+        p_scales_out(1)

@@ -53,13 +53,18 @@ def tile_clippedmatrixmechanismboundedrelease_x2_kernel(tc, g, r, a, c_words, c_
         q_scales = keep.tile([P, NCH, 2, W], U8, align_bytes=64)
         o_sb = keep.tile([P, 8, 1024], F32)
         ident = keep.tile([P, P], F32)
+        warm = keep.tile([P, 1], F32)
+        ps_all = keep.tile([P, 2, 1024], U8, align_bytes=64)
 
+        nc.vector.memset(warm[:], 1.0)
+        nc.scalar.activation(out=warm[:], in_=warm[:], func=ACT.Abs_reciprocal_sqrt)
         nc.vector.memset(cs_raw[:].rearrange("p g n -> p (g n)").bitcast(I32), 0)
         nc.gpsimd.dma_start(out=r_sb[:], in_=r.rearrange("(i p t) -> p i t", i=2, t=4))
         nc.gpsimd.dma_start(out=a_sb[:], in_=a.rearrange("(i p t) -> p i t", i=2, t=4))
         nc.gpsimd.dma_start(out=h_sb[:], in_=h.rearrange("(i p t) -> p i t", i=2, t=4))
         nc.gpsimd.memset(bs_sb[:].rearrange("p g n -> p (g n)").bitcast(I32), 0)
         make_identity(nc, ident[:])
+        nc.gpsimd.tensor_scalar(out=h2[:], in0=h_sb[:], scalar1=2.0, scalar2=0.0, op0=ALU.mult, op1=ALU.add)
 
         def load_words(dst, src, i):
             nc.sync.dma_start(out=dst[:, i, :].bitcast(I32), in_=src[i].bitcast(I32))
@@ -117,17 +122,19 @@ def tile_clippedmatrixmechanismboundedrelease_x2_kernel(tc, g, r, a, c_words, c_
 
         kc = {}
 
-        def k_scale(i, j0, width):
-            k_c = keep.tile([P, 4, 512], BF16, bufs=4)
-            for t in range(4):
+        def k_scale(i, j0, width, t0=0, t1=4):
+            if t0 == 0:
+                k_c = keep.tile([P, 4, 512], BF16, bufs=4)
+                for j in range(0, width, 256):
+                    kc[(i, (j0 + j) // 256)] = (k_c, j)
+            k_c = kc[(i, j0 // 256)][0]
+            for t in range(t0, t1):
                 nc.vector.tensor_scalar(
                     out=k_c[:, t, 0:width], in0=g_sb[:, i, t, j0 : j0 + width], scalar1=alpha[:, i, t : t + 1], scalar2=None, op0=ALU.mult
                 )
-            for j in range(0, width, 256):
-                kc[(i, (j0 + j) // 256)] = k_c[:, :, j : j + 256]
 
         def k_inter(qr, i):
-            nc.scalar.copy(out=ki[qr][:, i, :, :], in_=kc[(i, qr)].rearrange("p t j -> p j t"))
+            nc.scalar.copy(out=ki[qr][:, i, :, :], in_=kc[(i, qr)][0][:, :, kc[(i, qr)][1] : kc[(i, qr)][1] + 256].rearrange("p t j -> p j t"))
 
         def k_quant(qr, i0, i1):
             nc.vector.quantize_mx(
@@ -160,7 +167,7 @@ def tile_clippedmatrixmechanismboundedrelease_x2_kernel(tc, g, r, a, c_words, c_
 
         def noise(c):
             cols = slice(W * c, W * (c + 1))
-            e_sb = work.tile([P, 2, W, 4], F32)
+            e_sb = keep.tile([P, 2, W, 4], F32, bufs=3)
             et[c] = e_sb
             for b in range(2):
                 nc.vector.scalar_tensor_tensor(
@@ -175,14 +182,14 @@ def tile_clippedmatrixmechanismboundedrelease_x2_kernel(tc, g, r, a, c_words, c_
         th = {}
 
         def bound(c):
-            t_sb = work.tile([P, 2, W, 4], F32)
+            t_sb = keep.tile([P, 2, W, 4], F32, bufs=3)
             th[c] = t_sb
             nc.scalar.activation(out=t_sb[:], in_=et[c][:], func=ACT.Tanh, scale=0.5)
 
         qt = {}
 
         def gain(c):
-            q_sb = work.tile([P, 2, W, 4], BF16, align_bytes=64)
+            q_sb = keep.tile([P, 2, W, 4], BF16, align_bytes=64, bufs=3)
             qt[c] = q_sb
             nc.vector.tensor_tensor(out=q_sb[:], in0=th[c][:], in1=h2[:].unsqueeze(2).to_broadcast([P, 2, W, 4]), op=ALU.mult)
 
@@ -230,8 +237,7 @@ def tile_clippedmatrixmechanismboundedrelease_x2_kernel(tc, g, r, a, c_words, c_
             p_sb = work.tile([P, 8, 128, 4], BF16, align_bytes=64)
             pt[half] = p_sb
             p_codes = work.tile([P, 1024], U32, align_bytes=64)
-            p_scales = work.tile([P, 1024], U8, align_bytes=64)
-            pc[half] = (p_codes, p_scales)
+            pc[half] = (p_codes, ps_all[:, half, :])
 
         def turn_f32(half, v, on_vector=False):
             w_ps = pw.tile([P, 4, P], F32)
@@ -274,11 +280,12 @@ def tile_clippedmatrixmechanismboundedrelease_x2_kernel(tc, g, r, a, c_words, c_
             cols = slice(128 * v0, 128 * v1)
             nc.sync.dma_start(out=out_words[half].rearrange("p m t -> p (m t)").bitcast(I32)[:, cols], in_=pc[half][0][:, cols].bitcast(I32))
 
-        def p_scales_out(half):
+        def p_scales_out():
             for q4 in range(4):
-                nc.sync.dma_start(
-                    out=out_scales.bitcast(I32)[half, 4 * q4 : 4 * q4 + 4, :],
-                    in_=pc[half][1][32 * q4 : 32 * q4 + 4, :].bitcast(I32),
+                eng = nc.sync if q4 < 2 else nc.scalar
+                eng.dma_start(
+                    out=out_scales.bitcast(I32)[:, 4 * q4 : 4 * q4 + 4, :].rearrange("g q n -> q g n"),
+                    in_=ps_all[32 * q4 : 32 * q4 + 4, :, :].rearrange("p g n -> p (g n)").bitcast(I32).rearrange("p (g n) -> p g n", g=2),
                 )
 
         def c_order(i, b):
@@ -296,13 +303,13 @@ def tile_clippedmatrixmechanismboundedrelease_x2_kernel(tc, g, r, a, c_words, c_
             )
 
         def norm_root(i):
-            nc.scalar.activation(out=rn[:, i, :], in_=ss[:, i, :], func=ACT.Abs_reciprocal_sqrt, bias=1e-6)
+            nc.scalar.activation(out=ratio[:, i, :], in_=ss[:, i, :], func=ACT.Abs_reciprocal_sqrt, bias=1e-6)
 
         def norm_ratio(i):
-            nc.vector.tensor_tensor(out=ratio[:, i, :], in0=rn[:, i, :], in1=r_sb[:, i, :], op=ALU.mult)
+            nc.vector.tensor_tensor(out=rn[:, i, :], in0=ratio[:, i, :], in1=r_sb[:, i, :], op=ALU.mult)
 
         def norm_alpha(i):
-            nc.vector.scalar_tensor_tensor(out=alpha[:, i, :], in0=ratio[:, i, :], scalar=1.0, in1=a_sb[:, i, :], op0=ALU.min, op1=ALU.mult)
+            nc.vector.scalar_tensor_tensor(out=alpha[:, i, :], in0=rn[:, i, :], scalar=1.0, in1=a_sb[:, i, :], op0=ALU.min, op1=ALU.mult)
 
         c_order(0, 0)
         sumsq_s(0, 0)
@@ -310,36 +317,35 @@ def tile_clippedmatrixmechanismboundedrelease_x2_kernel(tc, g, r, a, c_words, c_
         sumsq_s(0, 2)
         sumsq_v(0, 3)
         c_order(0, 1)
-        norm_root(0)
         sumsq_s(1, 0)
-        norm_ratio(0)
-        sumsq_v(1, 2)
-        norm_alpha(0)
+        norm_root(0)
         sumsq_s(1, 1)
+        sumsq_v(1, 2)
         sumsq_s(1, 3)
         norm_root(1)
-        nc.vector.tensor_scalar(out=h2[:], in0=h_sb[:], scalar1=2.0, scalar2=None, op0=ALU.mult)
+        nc.scalar.activation(out=warm[:], in_=warm[:], func=ACT.Tanh)
+        norm_ratio(0)
+        c_order(1, 0)
+        norm_alpha(0)
+        cs_order(0)
         k_tile(0)
         k_tile(1)
         k_tile(2)
         k_tile(3)
         k_fused(0, 0)
-        c_order(1, 0)
         norm_ratio(1)
-        cs_order(0)
+        c_order(1, 1)
         norm_alpha(1)
         k_quant(0, 0, 1)
         k_scale(1, 0, 512)
         k_inter(0, 1)
         k_scale(0, 256, 256)
-        c_order(1, 1)
         cs_order(1)
-        k_quant(0, 1, 2)
         k_scale(0, 512, 512)
+        k_quant(0, 1, 2)
         k_scale(1, 512, 512)
         k_inter(1, 1)
         k_inter(1, 0)
-        k_inter(2, 1)
         p_tile(0)
         p_tile(1)
         enc(0)
@@ -351,8 +357,6 @@ def tile_clippedmatrixmechanismboundedrelease_x2_kernel(tc, g, r, a, c_words, c_
                 k_quant(1, 0, 2)
             if s == 3:
                 k_quant(2, 0, 2)
-            if s == 4:
-                k_quant(3, 0, 2)
             if 1 <= s + 1 < NCH and s >= 1:
                 enc(s + 1)
             if s >= 3:
@@ -365,10 +369,12 @@ def tile_clippedmatrixmechanismboundedrelease_x2_kernel(tc, g, r, a, c_words, c_
                 q_quant(s - 2)
                 dec(s - 2, 0)
                 dec(s - 2, 1)
-            if s in (0, 1, 2):
-                k_inter(*((3, 0), (2, 0), (3, 1))[s])
+            if s < 4:
+                k_inter(2 + s // 2, s % 2)
             if s >= 1:
                 gain(s - 1)
+            if s == 4:
+                k_quant(3, 0, 2)
             if s in (4, 6):
                 store(W * (s - 4), W * (s - 2))
         cast(4, 0, 2)
@@ -391,11 +397,11 @@ def tile_clippedmatrixmechanismboundedrelease_x2_kernel(tc, g, r, a, c_words, c_
         turn_f32(0, 3, True)
         dec(7, 1)
         cast(7, 0, 1)
+        store(W * 6, W * 7)
         turn_f32(0, 4)
         p_quant(0, 0, 4)
         p_store(0, 0, 4)
         leave(7, 1, True)
-        store(W * 6, W * 7)
         turn_f32(0, 5)
         turn_words(1, 0)
         turn_words(1, 1)
@@ -408,9 +414,8 @@ def tile_clippedmatrixmechanismboundedrelease_x2_kernel(tc, g, r, a, c_words, c_
         p_store(1, 0, 4)
         p_quant(0, 4, 8)
         p_store(0, 4, 8)
-        p_scales_out(0)
         turn_words(1, 2, True)
         turn_words(1, 3)
         p_quant(1, 4, 8)
         p_store(1, 4, 8)
-        p_scales_out(1)
+        p_scales_out()

@@ -25,9 +25,9 @@ def tile_clippedmatrixmechanismboundedrelease_x2_kernel(tc, g, r, a, c_words, c_
     with ExitStack() as ctx:
         keep = ctx.enter_context(tc.tile_pool(name="keep", bufs=1))
         work = ctx.enter_context(tc.tile_pool(name="work", bufs=2))
-        pe = ctx.enter_context(tc.psum_pool(name="pe", bufs=3))
+        pe = ctx.enter_context(tc.psum_pool(name="pe", bufs=4))
         pr = ctx.enter_context(tc.psum_pool(name="pr", bufs=2))
-        pw = ctx.enter_context(tc.psum_pool(name="pw", bufs=3))
+        pw = ctx.enter_context(tc.psum_pool(name="pw", bufs=2))
         ctx.enter_context(nc.allow_non_contiguous_dma(reason="small vectors and strided tiles"))
         ctx.enter_context(tc.manual_schedule())
 
@@ -51,7 +51,6 @@ def tile_clippedmatrixmechanismboundedrelease_x2_kernel(tc, g, r, a, c_words, c_
         k_scales = keep.tile([P, 4, 2, 256], U8, align_bytes=64)
         q_codes = keep.tile([P, NCH, 2, W], U32, align_bytes=64)
         q_scales = keep.tile([P, NCH, 2, W], U8, align_bytes=64)
-        o_sb = keep.tile([P, 8, 1024], F32)
         ident = keep.tile([P, P], F32)
         warm = keep.tile([P, 1], F32)
         ps_all = keep.tile([P, 2, 1024], U8, align_bytes=64)
@@ -218,8 +217,23 @@ def tile_clippedmatrixmechanismboundedrelease_x2_kernel(tc, g, r, a, c_words, c_
                         stop=(b == 1),
                     )
 
+        ot = {}
+
+        def o_tile(c):
+            if c < 6 and c % 2 == 0:
+                o_pair = keep.tile([P, 8, 2 * W], F32, bufs=3)
+                ot[c] = o_pair[:, :, 0:W]
+                ot[c + 1] = o_pair[:, :, W : 2 * W]
+                ot[(c, c + 1)] = o_pair
+            elif c >= 6:
+                o_one = keep.tile([P, 8, W], F32, bufs=2)
+                ot[c] = o_one[:]
+                ot[(c,)] = o_one
+
         def leave(c, u, on_vector=False):
-            dst = o_sb[:, 4 * u : 4 * u + 4, W * c : W * (c + 1)]
+            if u == 0:
+                o_tile(c)
+            dst = ot[c][:, 4 * u : 4 * u + 4, :]
             if on_vector:
                 nc.vector.tensor_copy(out=dst, in_=rb[(c, u)][:])
             else:
@@ -227,8 +241,9 @@ def tile_clippedmatrixmechanismboundedrelease_x2_kernel(tc, g, r, a, c_words, c_
 
         out3 = out.rearrange("(v p) j -> p v j", p=P)
 
-        def store(j0, j1, v0=0, v1=8):
-            nc.sync.dma_start(out=out3[:, v0:v1, j0:j1], in_=o_sb[:, v0:v1, j0:j1])
+        def store(j0, j1):
+            chunks = tuple(range(j0 // W, j1 // W))
+            nc.sync.dma_start(out=out3[:, :, j0:j1], in_=ot[chunks][:])
 
         pt = {}
         pc = {}
@@ -239,31 +254,35 @@ def tile_clippedmatrixmechanismboundedrelease_x2_kernel(tc, g, r, a, c_words, c_
             p_codes = work.tile([P, 1024], U32, align_bytes=64)
             pc[half] = (p_codes, ps_all[:, half, :])
 
-        def turn_f32(half, v, on_vector=False):
-            w_ps = pw.tile([P, 4, P], F32)
-            for t in range(4):
-                nc.tensor.transpose(w_ps[:, t, :], o_sb[:, v, 512 * half + t : 512 * (half + 1) : 4], ident[:])
-            dst = pt[half][:, v, :, :]
-            src = w_ps[:].rearrange("p t m -> p m t")
-            if on_vector:
-                nc.vector.tensor_copy(out=dst, in_=src)
-            else:
-                nc.scalar.copy(out=dst, in_=src)
-
-        o_bf = keep.tile([P, 8, 512], BF16)
+        ob = {}
 
         def cast(c, u0, u1):
-            j0 = W * (c % 4)
-            nc.vector.tensor_copy(out=o_bf[:, 4 * u0 : 4 * u1, j0 : j0 + W], in_=o_sb[:, 4 * u0 : 4 * u1, W * c : W * (c + 1)])
+            if c % 4 == 0 and u0 == 0:
+                o_bf = keep.tile([P, 8, 2, 128, 2], BF16, bufs=2)
+                ob[c // 4] = o_bf
+            p0 = 32 * (c % 4)
+            nc.vector.tensor_copy(
+                out=ob[c // 4][:, 4 * u0 : 4 * u1, :, p0 : p0 + 32, :],
+                in_=ot[c][:, 4 * u0 : 4 * u1, :].rearrange("r v (p u e) -> r v u p e", u=2, e=2),
+            )
 
-        def turn_words(half, v2, on_vector=False):
-            words = o_bf[:].bitcast(F32)
-            w_ps = pw.tile([P, 4, P], F32)
+        wb = {}
+
+        def turn(half, v2):
+            words = ob[half][:].rearrange("r v u p e -> r v u (p e)").bitcast(F32)
+            if half == 0:
+                w_ps = pw.tile([P, 4, P], F32)
+            else:
+                e_ps = pe.tile([P, 4, P], F32)
+                w_ps = e_ps
+            wb[(half, v2)] = w_ps
             for v in range(2):
                 for e in range(2):
-                    nc.tensor.transpose(w_ps[:, 2 * v + e, :], words[:, 2 * v2 + v, e::2], ident[:])
+                    nc.tensor.transpose(w_ps[:, 2 * v + e, :], words[:, 2 * v2 + v, e, :], ident[:])
+
+        def turned(half, v2, on_vector=False):
             dst = pt[half][:, 2 * v2 : 2 * v2 + 2, :, :].rearrange("p v m t -> p (v m t)").bitcast(F32).rearrange("p (v m e) -> p v m e", v=2, e=2)
-            src = w_ps[:].rearrange("p (v e) m -> p v m e", v=2)
+            src = wb[(half, v2)][:].rearrange("p (v e) m -> p v m e", v=2)
             if on_vector:
                 nc.vector.tensor_copy(out=dst, in_=src)
             else:
@@ -348,6 +367,13 @@ def tile_clippedmatrixmechanismboundedrelease_x2_kernel(tc, g, r, a, c_words, c_
         k_inter(1, 0)
         p_tile(0)
         p_tile(1)
+        def wake():
+            w_ps = pw.tile([P, 4, P], F32)
+            scaled = ki[0][:, 0, :, :].rearrange("p j t -> p (j t)")
+            for x in range(8):
+                nc.tensor.matmul(out=w_ps[:].rearrange("p a b -> p (a b)"), lhsT=scaled[:, 0:P], rhs=scaled[:, 0:512], start=True, stop=True)
+
+        wake()
         enc(0)
         enc(1)
 
@@ -363,8 +389,6 @@ def tile_clippedmatrixmechanismboundedrelease_x2_kernel(tc, g, r, a, c_words, c_
                 leave(s - 3, 0)
                 leave(s - 3, 1)
             bound(s)
-            if s == 6:
-                turn_f32(0, 0)
             if s >= 2:
                 q_quant(s - 2)
                 dec(s - 2, 0)
@@ -377,45 +401,56 @@ def tile_clippedmatrixmechanismboundedrelease_x2_kernel(tc, g, r, a, c_words, c_
                 k_quant(3, 0, 2)
             if s in (4, 6):
                 store(W * (s - 4), W * (s - 2))
-        cast(4, 0, 2)
         leave(5, 0)
         leave(5, 1)
-        turn_f32(0, 1)
+        cast(0, 0, 2)
         q_quant(6)
         dec(6, 0)
-        gain(7)
-        q_quant(7)
-        leave(6, 0)
-        turn_f32(0, 2, True)
         dec(6, 1)
+        gain(7)
+        cast(1, 0, 1)
+        q_quant(7)
+        cast(1, 1, 2)
+        cast(2, 0, 2)
+        cast(3, 0, 2)
+        leave(6, 0)
         leave(6, 1)
         dec(7, 0)
-        leave(7, 0)
-        store(W * 4, W * 6)
-        cast(5, 0, 2)
-        cast(6, 0, 1)
-        turn_f32(0, 3, True)
         dec(7, 1)
-        cast(7, 0, 1)
+        store(W * 4, W * 6)
+        turn(0, 0)
+        turn(0, 1)
+        leave(7, 0)
+        leave(7, 1)
         store(W * 6, W * 7)
-        turn_f32(0, 4)
-        p_quant(0, 0, 4)
-        p_store(0, 0, 4)
-        leave(7, 1, True)
-        turn_f32(0, 5)
-        turn_words(1, 0)
-        turn_words(1, 1)
-        cast(6, 1, 2)
+        cast(4, 0, 2)
+        cast(5, 0, 2)
+        cast(6, 0, 2)
+        turned(0, 0)
+        turned(0, 1)
+        turn(0, 2)
+        cast(7, 0, 1)
         cast(7, 1, 2)
         store(W * 7, W * 8)
-        turn_f32(0, 6, True)
-        turn_f32(0, 7)
+        turn(1, 0)
+        turn(1, 1)
+        turn(1, 2)
+        turn(1, 3)
+        turn(0, 3)
+        p_quant(0, 0, 4)
+        p_store(0, 0, 4)
+        turned(0, 2)
+        turned(1, 0)
+        turned(1, 1, True)
+        turned(1, 2, True)
+        turned(1, 3)
         p_quant(1, 0, 4)
         p_store(1, 0, 4)
-        p_quant(0, 4, 8)
-        p_store(0, 4, 8)
-        turn_words(1, 2, True)
-        turn_words(1, 3)
         p_quant(1, 4, 8)
         p_store(1, 4, 8)
+        turned(0, 3)
+        p_quant(0, 4, 6)
+        p_store(0, 4, 6)
+        p_quant(0, 6, 8)
+        p_store(0, 6, 8)
         p_scales_out()

from contextlib import ExitStack

import concourse.mybir as mybir
from concourse.masks import make_identity

F32 = mybir.dt.float32
BF16 = mybir.dt.bfloat16
U32 = mybir.dt.uint32
I32 = mybir.dt.int32
U8 = mybir.dt.uint8
E4M3 = mybir.dt.float8_e4m3fn_x4
E2M1 = mybir.dt.float4_e2m1fn_x4
ACT = mybir.ActivationFunctionType
ALU = mybir.AluOpType

FLOPS = 2 * 2 * 1024 * 1024 * 1024

P = 128
W = 128
NCH = 8


def tile_clippedmatrixmechanismboundedrelease_x2_kernel(tc, g, r, a, c_words, c_scales, z, h, b_words, b_scales, out, out_words, out_scales):
    nc = tc.nc
    with ExitStack() as ctx:
        keep = ctx.enter_context(tc.tile_pool(name="keep", bufs=1))
        work = ctx.enter_context(tc.tile_pool(name="work", bufs=2))
        pe = ctx.enter_context(tc.psum_pool(name="pe", bufs=4))
        pr = ctx.enter_context(tc.psum_pool(name="pr", bufs=2))
        pw = ctx.enter_context(tc.psum_pool(name="pw", bufs=2))
        ctx.enter_context(nc.allow_non_contiguous_dma(reason="small vectors and strided tiles"))
        ctx.enter_context(tc.manual_schedule())

        g_sb = keep.tile([P, 2, 4, 1024], BF16)
        c_raw = keep.tile([P, 2, 2048], U8, align_bytes=64)
        c_perm = keep.tile([P, 2, 2048], U8, align_bytes=64)
        cs_raw = keep.tile([P, 2, 1024], U8, align_bytes=64)
        cs_perm = keep.tile([P, 2, 1024], U8, align_bytes=64)
        b_sb = keep.tile([P, 2, 2048], U8, align_bytes=64)
        bs_sb = keep.tile([P, 2, 1024], U8, align_bytes=64)
        z_sb = keep.tile([P, 2, 4, 1024], BF16)
        r_sb = keep.tile([P, 2, 4], BF16)
        a_sb = keep.tile([P, 2, 4], BF16)
        h_sb = keep.tile([P, 2, 4], BF16)
        h2 = keep.tile([P, 2, 4], F32)
        ss = keep.tile([P, 2, 4], F32)
        rn = keep.tile([P, 2, 4], F32)
        ratio = keep.tile([P, 2, 4], F32)
        alpha = keep.tile([P, 2, 4], F32)
        k_codes = keep.tile([P, 4, 2, 256], U32, align_bytes=64)
        k_scales = keep.tile([P, 4, 2, 256], U8, align_bytes=64)
        q_codes = keep.tile([P, NCH, 2, W], U32, align_bytes=64)
        q_scales = keep.tile([P, NCH, 2, W], U8, align_bytes=64)
        ident = keep.tile([P, P], F32)
        warm = keep.tile([P, 1], F32)
        ps_all = keep.tile([P, 2, 1024], U8, align_bytes=64)

        nc.vector.memset(warm[:], 1.0)
        nc.scalar.activation(out=warm[:], in_=warm[:], func=ACT.Abs_reciprocal_sqrt)
        nc.vector.memset(cs_raw[:].rearrange("p g n -> p (g n)").bitcast(I32), 0)
        nc.gpsimd.dma_start(out=r_sb[:], in_=r.rearrange("(i p t) -> p i t", i=2, t=4))
        nc.gpsimd.dma_start(out=a_sb[:], in_=a.rearrange("(i p t) -> p i t", i=2, t=4))
        nc.gpsimd.dma_start(out=h_sb[:], in_=h.rearrange("(i p t) -> p i t", i=2, t=4))
        nc.gpsimd.memset(bs_sb[:].rearrange("p g n -> p (g n)").bitcast(I32), 0)
        make_identity(nc, ident[:])
        nc.gpsimd.tensor_scalar(out=h2[:], in0=h_sb[:], scalar1=2.0, scalar2=0.0, op0=ALU.mult, op1=ALU.add)

        def load_words(dst, src, i):
            nc.sync.dma_start(out=dst[:, i, :].bitcast(I32), in_=src[i].bitcast(I32))

        def load_scales(dst, src):
            for q4 in range(4):
                nc.sync.dma_start(
                    out=dst[32 * q4 : 32 * q4 + 4, :, :].rearrange("p g n -> p (g n)").bitcast(I32).rearrange("p (g n) -> p g n", g=2),
                    in_=src.bitcast(I32)[:, 4 * q4 : 4 * q4 + 4, :].rearrange("g q n -> q g n"),
                )

        g4 = g.rearrange("(i p t) j -> i p t j", i=2, t=4)
        z4 = z.rearrange("(i p t) j -> p i t j", i=2, t=4)
        load_words(c_raw, c_words, 0)
        for i, t0, t1 in [(0, 0, 1), (0, 1, 2), (0, 2, 4), (1, 0, 2), (1, 2, 4)]:
            nc.sync.dma_start(out=g_sb[:, i, t0:t1, :], in_=g4[i, :, t0:t1, :])
        load_words(c_raw, c_words, 1)
        load_scales(cs_raw, c_scales)
        for i in range(2):
            nc.sync.dma_start(out=z_sb[:, i, :, 0:512], in_=z4[:, i, :, 0:512])
        for i in range(2):
            load_words(b_sb, b_words, i)
        load_scales(bs_sb, b_scales)
        for i in range(2):
            nc.sync.dma_start(out=z_sb[:, i, :, 512:1024], in_=z4[:, i, :, 512:1024])

        def sumsq_s(i, t):
            sq_s = work.tile([P, 1024], BF16)
            nc.scalar.activation(out=sq_s[:], in_=g_sb[:, i, t, :], func=ACT.Square, accum_out=ss[:, i, t : t + 1])

        def sumsq_v(i, t):
            sq_v = work.tile([P, 1024], F32)
            nc.vector.scalar_tensor_tensor(
                out=sq_v[:], in0=g_sb[:, i, t, :], scalar=1.0, in1=g_sb[:, i, t, :], op0=ALU.mult, op1=ALU.mult, accum_out=ss[:, i, t : t + 1]
            )

        def norms(i):
            nc.scalar.activation(out=rn[:, i, :], in_=ss[:, i, :], func=ACT.Abs_reciprocal_sqrt, bias=1e-6)
            nc.vector.tensor_tensor(out=ratio[:, i, :], in0=rn[:, i, :], in1=r_sb[:, i, :], op=ALU.mult)
            nc.vector.scalar_tensor_tensor(out=alpha[:, i, :], in0=ratio[:, i, :], scalar=1.0, in1=a_sb[:, i, :], op0=ALU.min, op1=ALU.mult)

        ki = {}

        def k_tile(qr):
            k_in = keep.tile([P, 2, 256, 4], BF16, align_bytes=64, bufs=4)
            ki[qr] = k_in

        def k_fused(qr, i):
            nc.vector.tensor_tensor(
                out=ki[qr][:, i, :, :],
                in0=g_sb[:, i, :, 256 * qr : 256 * (qr + 1)].rearrange("p t j -> p j t"),
                in1=alpha[:, i, :].unsqueeze(1).to_broadcast([P, 256, 4]),
                op=ALU.mult,
            )

        kc = {}

        def k_scale(i, j0, width, t0=0, t1=4):
            if t0 == 0:
                k_c = keep.tile([P, 4, 512], BF16, bufs=4)
                for j in range(0, width, 256):
                    kc[(i, (j0 + j) // 256)] = (k_c, j)
            k_c = kc[(i, j0 // 256)][0]
            for t in range(t0, t1):
                nc.vector.tensor_scalar(
                    out=k_c[:, t, 0:width], in0=g_sb[:, i, t, j0 : j0 + width], scalar1=alpha[:, i, t : t + 1], scalar2=None, op0=ALU.mult
                )

        def k_inter(qr, i):
            nc.scalar.copy(out=ki[qr][:, i, :, :], in_=kc[(i, qr)][0][:, :, kc[(i, qr)][1] : kc[(i, qr)][1] + 256].rearrange("p t j -> p j t"))

        def k_quant(qr, i0, i1):
            nc.vector.quantize_mx(
                out=k_codes[:, qr, i0:i1, :].rearrange("p i j -> p (i j)").bitcast(E4M3),
                scales=k_scales[:, qr, i0:i1, :].rearrange("p i j -> p (i j)"),
                in_=ki[qr][:, i0:i1, :, :].rearrange("p i j t -> p (i j t)"),
            )

        eb = {}

        def enc(c):
            cols = slice(W * (c % 2), W * (c % 2 + 1))
            for b in range(2):
                e_ps = pe.tile([P, 4, W], F32)
                eb[(c, b)] = e_ps
                for t in range(4):
                    m0 = 512 * b + 128 * t
                    for i in range(2):
                        nc.tensor.matmul_mx(
                            out=e_ps[:, t, :],
                            lhsT=c_perm[:, i, 2 * m0 : 2 * m0 + 256].bitcast(E2M1),
                            lhsT_scale=cs_perm[:, i, m0 : m0 + 128],
                            rhs=k_codes[:, c // 2, i, cols].bitcast(E4M3),
                            rhs_scale=k_scales[:, c // 2, i, cols],
                            start=(i == 0),
                            stop=(i == 1),
                        )

        et = {}

        def noise(c):
            cols = slice(W * c, W * (c + 1))
            e_sb = keep.tile([P, 2, W, 4], F32, bufs=3)
            et[c] = e_sb
            for b in range(2):
                nc.vector.scalar_tensor_tensor(
                    out=e_sb[:, b, :, :],
                    in0=z_sb[:, b, :, cols].rearrange("p t j -> p j t"),
                    scalar=0.5,
                    in1=eb[(c, b)][:].rearrange("p t j -> p j t"),
                    op0=ALU.mult,
                    op1=ALU.add,
                )

        th = {}

        def bound(c):
            t_sb = keep.tile([P, 2, W, 4], F32, bufs=3)
            th[c] = t_sb
            nc.scalar.activation(out=t_sb[:], in_=et[c][:], func=ACT.Tanh, scale=0.5)

        qt = {}

        def gain(c):
            q_sb = keep.tile([P, 2, W, 4], BF16, align_bytes=64, bufs=3)
            qt[c] = q_sb
            nc.vector.tensor_tensor(out=q_sb[:], in0=th[c][:], in1=h2[:].unsqueeze(2).to_broadcast([P, 2, W, 4]), op=ALU.mult)

        def q_quant(c):
            nc.vector.quantize_mx(
                out=q_codes[:, c, :, :].rearrange("p b j -> p (b j)").bitcast(E4M3),
                scales=q_scales[:, c, :, :].rearrange("p b j -> p (b j)"),
                in_=qt[c][:].rearrange("p b j t -> p (b j t)"),
            )

        rb = {}

        def dec(c, u):
            r_ps = pr.tile([P, 4, W], F32)
            rb[(c, u)] = r_ps
            for v in range(4):
                n0 = 128 * (4 * u + v)
                for b in range(2):
                    nc.tensor.matmul_mx(
                        out=r_ps[:, v, :],
                        lhsT=b_sb[:, b, 2 * n0 : 2 * n0 + 256].bitcast(E2M1),
                        lhsT_scale=bs_sb[:, b, n0 : n0 + 128],
                        rhs=q_codes[:, c, b, :].bitcast(E4M3),
                        rhs_scale=q_scales[:, c, b, :],
                        start=(b == 0),
                        stop=(b == 1),
                    )

        ot = {}

        def o_tile(c):
            if c < 6 and c % 2 == 0:
                o_pair = keep.tile([P, 8, 2 * W], F32, bufs=3)
                ot[c] = o_pair[:, :, 0:W]
                ot[c + 1] = o_pair[:, :, W : 2 * W]
                ot[(c, c + 1)] = o_pair
            elif c >= 6:
                o_one = keep.tile([P, 8, W], F32, bufs=2)
                ot[c] = o_one[:]
                ot[(c,)] = o_one

        def leave(c, u, on_vector=False):
            if u == 0:
                o_tile(c)
            dst = ot[c][:, 4 * u : 4 * u + 4, :]
            if on_vector:
                nc.vector.tensor_copy(out=dst, in_=rb[(c, u)][:])
            else:
                nc.scalar.copy(out=dst, in_=rb[(c, u)][:])

        out3 = out.rearrange("(v p) j -> p v j", p=P)

        def store(j0, j1):
            chunks = tuple(range(j0 // W, j1 // W))
            nc.sync.dma_start(out=out3[:, :, j0:j1], in_=ot[chunks][:])

        pt = {}
        pc = {}

        def p_tile(half):
            p_sb = work.tile([P, 8, 128, 4], BF16, align_bytes=64)
            pt[half] = p_sb
            p_codes = work.tile([P, 1024], U32, align_bytes=64)
            pc[half] = (p_codes, ps_all[:, half, :])

        ob = {}

        def cast(c, u0, u1):
            if c % 4 == 0 and u0 == 0:
                o_bf = keep.tile([P, 8, 2, 128, 2], BF16, bufs=2)
                ob[c // 4] = o_bf
            p0 = 32 * (c % 4)
            nc.vector.tensor_copy(
                out=ob[c // 4][:, 4 * u0 : 4 * u1, :, p0 : p0 + 32, :],
                in_=ot[c][:, 4 * u0 : 4 * u1, :].rearrange("r v (p u e) -> r v u p e", u=2, e=2),
            )

        wb = {}

        def turn(half, v2):
            words = ob[half][:].rearrange("r v u p e -> r v u (p e)").bitcast(F32)
            if half == 0:
                w_ps = pw.tile([P, 4, P], F32)
            else:
                e_ps = pe.tile([P, 4, P], F32)
                w_ps = e_ps
            wb[(half, v2)] = w_ps
            for v in range(2):
                for e in range(2):
                    nc.tensor.transpose(w_ps[:, 2 * v + e, :], words[:, 2 * v2 + v, e, :], ident[:])

        def turned(half, v2, on_vector=False):
            dst = pt[half][:, 2 * v2 : 2 * v2 + 2, :, :].rearrange("p v m t -> p (v m t)").bitcast(F32).rearrange("p (v m e) -> p v m e", v=2, e=2)
            src = wb[(half, v2)][:].rearrange("p (v e) m -> p v m e", v=2)
            if on_vector:
                nc.vector.tensor_copy(out=dst, in_=src)
            else:
                nc.scalar.copy(out=dst, in_=src)

        def p_quant(half, v0, v1):
            codes, scales = pc[half]
            cols = slice(128 * v0, 128 * v1)
            nc.vector.quantize_mx(
                out=codes[:, cols].bitcast(E4M3), scales=scales[:, cols], in_=pt[half][:, v0:v1, :, :].rearrange("p v m t -> p (v m t)")
            )

        def p_store(half, v0, v1):
            cols = slice(128 * v0, 128 * v1)
            nc.sync.dma_start(out=out_words[half].rearrange("p m t -> p (m t)").bitcast(I32)[:, cols], in_=pc[half][0][:, cols].bitcast(I32))

        def p_scales_out():
            for q4 in range(4):
                eng = nc.sync if q4 < 2 else nc.scalar
                eng.dma_start(
                    out=out_scales.bitcast(I32)[:, 4 * q4 : 4 * q4 + 4, :].rearrange("g q n -> q g n"),
                    in_=ps_all[32 * q4 : 32 * q4 + 4, :, :].rearrange("p g n -> p (g n)").bitcast(I32).rearrange("p (g n) -> p g n", g=2),
                )

        def c_order(i, b):
            cols = slice(1024 * b, 1024 * (b + 1))
            nc.vector.tensor_copy(
                out=c_perm[:, i, cols].rearrange("p (t q e) -> p t q e", t=4, e=2),
                in_=c_raw[:, i, cols].rearrange("p (q t e) -> p t q e", t=4, e=2),
            )

        def cs_order(b):
            cols = slice(512 * b, 512 * (b + 1))
            nc.vector.tensor_copy(
                out=cs_perm[:, :, cols].rearrange("p i (t q) -> p i t q", t=4),
                in_=cs_raw[:, :, cols].rearrange("p i (q t) -> p i t q", t=4),
            )

        def norm_root(i):
            nc.scalar.activation(out=ratio[:, i, :], in_=ss[:, i, :], func=ACT.Abs_reciprocal_sqrt, bias=1e-6)

        def norm_ratio(i):
            nc.vector.tensor_tensor(out=rn[:, i, :], in0=ratio[:, i, :], in1=r_sb[:, i, :], op=ALU.mult)

        def norm_alpha(i):
            nc.vector.scalar_tensor_tensor(out=alpha[:, i, :], in0=rn[:, i, :], scalar=1.0, in1=a_sb[:, i, :], op0=ALU.min, op1=ALU.mult)

        c_order(0, 0)
        sumsq_s(0, 0)
        sumsq_v(0, 1)
        sumsq_s(0, 2)
        sumsq_v(0, 3)
        c_order(0, 1)
        sumsq_s(1, 0)
        norm_root(0)
        sumsq_s(1, 1)
        sumsq_v(1, 2)
        sumsq_s(1, 3)
        norm_root(1)
        nc.scalar.activation(out=warm[:], in_=warm[:], func=ACT.Tanh)
        norm_ratio(0)
        c_order(1, 0)
        norm_alpha(0)
        cs_order(0)
        k_tile(0)
        k_tile(1)
        k_tile(2)
        k_tile(3)
        k_fused(0, 0)
        norm_ratio(1)
        c_order(1, 1)
        norm_alpha(1)
        k_quant(0, 0, 1)
        k_scale(1, 0, 512)
        k_inter(0, 1)
        k_scale(0, 256, 256)
        cs_order(1)
        k_scale(0, 512, 512)
        k_quant(0, 1, 2)
        k_scale(1, 512, 512)
        k_inter(1, 1)
        k_inter(1, 0)
        p_tile(0)
        p_tile(1)
        def wake():
            w_ps = pw.tile([P, 4, P], F32)
            scaled = ki[0][:, 0, :, :].rearrange("p j t -> p (j t)")
            for x in range(8):
                nc.tensor.matmul(out=w_ps[:].rearrange("p a b -> p (a b)"), lhsT=scaled[:, 0:P], rhs=scaled[:, 0:512], start=True, stop=True)

        wake()
        enc(0)
        enc(1)

        for s in range(0, 8):
            noise(s)
            if s == 0:
                k_quant(1, 0, 2)
            if s == 3:
                k_quant(2, 0, 2)
            if 1 <= s + 1 < NCH and s >= 1:
                enc(s + 1)
            if s >= 3:
                leave(s - 3, 0)
                leave(s - 3, 1)
            bound(s)
            if s >= 2:
                q_quant(s - 2)
                dec(s - 2, 0)
                dec(s - 2, 1)
            if s < 4:
                k_inter(2 + s // 2, s % 2)
            if s >= 1:
                gain(s - 1)
            if s == 4:
                k_quant(3, 0, 2)
            if s in (4, 6):
                store(W * (s - 4), W * (s - 2))
        leave(5, 0)
        leave(5, 1)
        cast(0, 0, 2)
        q_quant(6)
        dec(6, 0)
        dec(6, 1)
        gain(7)
        cast(1, 0, 1)
        q_quant(7)
        cast(1, 1, 2)
        cast(2, 0, 2)
        cast(3, 0, 2)
        leave(6, 0)
        leave(6, 1)
        dec(7, 0)
        dec(7, 1)
        store(W * 4, W * 6)
        turn(0, 0)
        turn(0, 1)
        leave(7, 0)
        leave(7, 1)
        store(W * 6, W * 7)
        cast(4, 0, 2)
        cast(5, 0, 2)
        cast(6, 0, 2)
        turned(0, 0)
        turned(0, 1)
        turn(0, 2)
        cast(7, 0, 1)
        cast(7, 1, 2)
        store(W * 7, W * 8)
        turn(1, 0)
        turn(1, 1)
        turn(1, 2)
        turn(1, 3)
        turn(0, 3)
        p_quant(0, 0, 4)
        p_store(0, 0, 4)
        turned(0, 2)
        turned(1, 0)
        turned(1, 1, True)
        turned(1, 2, True)
        turned(1, 3)
        p_quant(1, 0, 4)
        p_store(1, 0, 4)
        p_quant(1, 4, 8)
        p_store(1, 4, 8)
        turned(0, 3)
        p_quant(0, 4, 6)
        p_store(0, 4, 6)
        p_quant(0, 6, 8)
        p_store(0, 6, 8)
        p_scales_out()
